import numpy as np, ml_dtypes
CORES = [66,74,82,90,194,202,210,218]
N = 8
KB, QP = 2, 32
def setup_inputs(rng):
    q = rng.standard_normal((N, 128, QP), dtype=np.float32) / 4; k = rng.standard_normal((N, 128, KB * 128), dtype=np.float32)
    a = 2 * np.pi * rng.random((N, QP)); s = 400 * rng.random((N, QP)) ** 1.5; q[:, 0, :] = s * np.cos(a); q[:, 1, :] = s * np.sin(a); q[:, 2, :] = 150 * rng.standard_normal((N, QP)); k[:, 2, :] = 1 + k[:, 2, :] / 50
    a = (2 * np.pi * rng.random() + np.pi / 2 * (rng.permutation(N).reshape(N, 1, 1) + 0.5) / N - 0.5 + (np.arange(KB).reshape(1, KB, 1) + rng.random((N, KB, 128))) / KB).reshape(N, KB * 128); k[:, 0, :] = np.cos(a); k[:, 1, :] = np.sin(a)
    return {"q": q.astype(ml_dtypes.bfloat16), "k": k.astype(ml_dtypes.bfloat16), "v": rng.standard_normal((N, 128, KB * 128), dtype=np.float32).astype(ml_dtypes.bfloat16)}
def setup_inputs_big(rng):
    d = setup_inputs(rng)
    for k in ("v",): d[k] = (d[k].astype(np.float32) * 1048576.0).astype(d[k].dtype)
    return d
def setup_inputs_small(rng):
    d = setup_inputs(rng)
    for k in ("v",): d[k] = (d[k].astype(np.float32) * (1 / 1048576.0)).astype(d[k].dtype)
    return d
def reference(q, k, v):
    Q, K, V = q.astype(np.float64), k.astype(np.float64), v.astype(np.float64)
    y = np.zeros((N, QP, 128))
    for r in range(N):
        js = list(range(N))
        S = np.concatenate([K[j].T @ Q[r] for j in js], axis=0)
        P = np.exp(S - S.max(axis=0)); P = P / P.sum(axis=0)
        y[r] = P.T @ np.concatenate([V[j][:, 128 * b:128 * b + 128] for j in js for b in range(KB)], axis=0)
    return {"y": y.astype(ml_dtypes.bfloat16)}

@@ -1,0 +1,220 @@
+from concourse.bass import DstId, RemoteDMATransfer
+from concourse.mybir import AluOpType, AxisListType, ActivationFunctionType
+
+QP = 32
+MW = 2 * QP
+STAGES = [(0,), (1,), (2, 3), (4, 5), (6, 7)]
+NS = len(STAGES)
+PRE_STAGES = 3
+NPRE = sum(len(o) for o in STAGES[:PRE_STAGES])
+
+SCRATCH = {
+    "qall": ("sbuf", [128, 256], "bfloat16"),
+    "kbuf": ("sbuf", [128, 256], "bfloat16"),
+    "vbuf": ("sbuf", [128, 256], "bfloat16"),
+    "ones": ("sbuf", [128, 128], "bfloat16"),
+    "onesa": ("sbuf", [128, 128], "bfloat16"),
+    "onesb": ("sbuf", [128, 128], "bfloat16"),
+    "ident": ("sbuf", [128, 128], "bfloat16"),
+    "negm": ("sbuf", [128, 8], "bfloat16"),
+    "diag": ("sbuf", [128, 256], "bfloat16"),
+    "pbuf": ("sbuf", [128, 512], "bfloat16"),
+    "send": ("sbuf", [128, 8, MW], "bfloat16"),
+    "land": ("sbuf", [128, 8, MW], "bfloat16"),
+    "t1": ("sbuf", [128, 8, MW], "bfloat16"),
+    "xp": ("sbuf", [128, 8, QP + 1], "float32"),
+    "xf": ("sbuf", [128, 8, QP + 1], "float32"),
+    "mnp": ("sbuf", [128, 1], "float32"),
+    "mnf": ("sbuf", [128, 1], "float32"),
+    "rl": ("sbuf", [128, 1], "float32"),
+    "yt": ("sbuf", [128, QP], "bfloat16"),
+    "st": ("psum", [128, 512], "float32"),
+    "sp0": ("psum", [128, 512], "float32"),
+    "sp1": ("psum", [128, 512], "float32"),
+    "ms0": ("psum", [128, 4, 128], "float32"),
+    "ms1": ("psum", [128, 4, 128], "float32"),
+    "wpp": ("psum", [128, 16, QP], "float32"),
+    "wpf": ("psum", [128, 16, QP], "float32"),
+}
+
+SEMAPHORES = (["ldq", "ldk", "ldv", "sones", "sfill", "smask", "sident", "lsem", "sacc", "srl", "syt", "sy"]
+              + ["%s%s" % (n, t) for t in "pf" for n in ("mn", "w", "x", "u0", "u1", "u2")]
+              + ["%s%d" % (n, s) for s in range(NS)
+                 for n in ("qa", "a", "r", "d", "ba", "bb", "ea", "eb", "c", "cp", "pa", "t")])
+
+
+def _split(mask, n):
+    bits = [b for b in range(mask.bit_length()) if (mask >> b) & 1]
+    per = len(bits) // n
+    return [sum(1 << b for b in bits[i * per:(i + 1) * per]) for i in range(n)], per
+
+
+def rank_program(g, core, T, topo):
+    j = T.rank_of(core)
+    if j is None:
+        return
+    pe, dve, act, sp = g.tensor, g.vector, g.scalar, g.sync
+    S = T.sem
+    Exp = ActivationFunctionType.Exp
+    X = AxisListType.X
+    mult, add = AluOpType.mult, AluOpType.add
+
+    def dst_id(r):
+        rid, pid = topo.addr(T.cores[r], core)
+        return DstId(rid=rid, pnc=pid)
+
+    def common_mask(rs):
+        m = topo.mask(core, T.cores[rs[0]])
+        for r in rs[1:]:
+            m &= topo.mask(core, T.cores[r])
+        return m
+
+    ranks = [sorted(j ^ o for o in offs) for offs in STAGES]
+    c0s = [QP * rs[0] for rs in ranks]
+    ws = [QP * len(rs) for rs in ranks]
+    myq = T.qall[:, QP * j:QP * j + QP]
+
+    sp.dma_start(myq, T.q[:, :]).then_inc(S.ldq, 16)
+    act.dma_start(T.kbuf[:, :], T.k[:, :]).then_inc(S.ldk, 16)
+    sp.dma_start(T.vbuf[:, :], T.v[:, :]).then_inc(S.ldv, 16)
+
+    dve.memset(T.ones[:, :], 1.0).then_inc(S.sones, 1)
+    dve.memset(T.onesa[:, :], 1.0).then_inc(S.sfill, 1)
+    dve.memset(T.onesb[:, :], 0.0).then_inc(S.sfill, 1)
+    dve.wait_ge(S.sfill, 2)
+    dve.memset(T.onesa[:, QP - 1::QP], 0.0).then_inc(S.smask, 1)
+    dve.memset(T.onesb[:, QP - 1::QP], 1.0).then_inc(S.smask, 1)
+    g.wait_ge(S.sones, 1)
+    g.affine_select(T.ident[:, :], T.ones[:, :], [[-1, 128]], AluOpType.is_equal, 0.0, 0, 1).then_inc(S.sident, 1)
+
+    lcount = 0
+    g.wait_ge(S.ldq, 16)
+    for s in range(1, NS):
+        rs = ranks[s]
+        m = common_mask(rs)
+        _, per = _split(m, 1)
+        g.remote_dma_fused([RemoteDMATransfer(dst_ids=[dst_id(r) for r in rs], dma_engine_mask=m,
+                                              remote_sem=S["qa%d" % s], srcs=[myq], dsts=[myq for r in rs])],
+                           local_sem=S.lsem)
+        lcount += per
+
+    for s in range(NS):
+        w, c0 = ws[s], c0s[s]
+        ms = T["ms%d" % (s % 2)]
+        qs = T.qall[:, c0:c0 + w]
+        dg = T.diag[0:w, c0:c0 + w]
+        if s == 0:
+            pe.wait_ge(S.ldq, 16)
+            pe.wait_ge(S.ldk, 16)
+        else:
+            _, per = _split(common_mask(ranks[s]), 1)
+            pe.wait_ge(S["qa%d" % s], per * len(ranks[s]))
+        pe.matmul(T.st[0:w, 0:256], qs, T.kbuf[:, :], True, True).then_inc(S["a%d" % s], 1)
+        for b, n in enumerate("ab"):
+            pe.matmul(T["sp%d" % b][:, 0:w], T.kbuf[:, 128 * b:128 * b + 128], qs, True, False).then_inc(S["b%s%d" % (n, s)], 1)
+        if s == 0:
+            pe.wait_ge(S.sones, 1)
+            pe.wait_ge(S.smask, 2)
+        pe.wait_ge(S["d%d" % s], 1)
+        for b, n in enumerate("ab"):
+            pe.matmul(T["sp%d" % b][:, 0:w], T.ones[0:w, :], dg, False, True).then_inc(S["b%s%d" % (n, s)], 1)
+        if s >= 2:
+            pe.wait_ge(S["cp%d" % (s - 2)], len(ranks[s - 2]))
+        pe.matmul(ms[:, 1, 0:w], T.onesa[0:w, :], dg, True, False).then_inc(S["c%d" % s], 1)
+        for b, n in enumerate("ab"):
+            pe.wait_ge(S["e%s%d" % (n, s)], 1)
+            pe.matmul(ms[:, 1, 0:w], T.onesb[:, :], T.pbuf[:, 2 * c0 + b * w:2 * c0 + (b + 1) * w],
+                      False, b == 1).then_inc(S["c%d" % s], 1)
+        if s == 0:
+            pe.wait_ge(S.ldv, 16)
+        for b in range(2):
+            pe.matmul(ms[:, 0, 0:w], T.vbuf[:, 128 * b:128 * b + 128], T.pbuf[:, 2 * c0 + b * w:2 * c0 + (b + 1) * w],
+                      b == 0, b == 1).then_inc(S["c%d" % s], 1)
+
+    for s in range(NS):
+        w, c0 = ws[s], c0s[s]
+        for b, n in enumerate("ab"):
+            act.wait_ge(S["b%s%d" % (n, s)], 2)
+            act.activation(T.pbuf[:, 2 * c0 + b * w:2 * c0 + (b + 1) * w], T["sp%d" % b][:, 0:w],
+                           Exp).then_inc(S["e%s%d" % (n, s)], 1)
+
+    for s in range(NS):
+        w, c0 = ws[s], c0s[s]
+        ms = T["ms%d" % (s % 2)]
+        dve.wait_ge(S["a%d" % s], 1)
+        dve.tensor_reduce(T.negm[0:w, s:s + 1], T.st[0:w, 0:256], axis=X, op=AluOpType.max,
+                          negate=True).then_inc(S["r%d" % s], 1)
+        dve.wait_ge(S["r%d" % s], 1)
+        if s == 0:
+            dve.wait_ge(S.sident, 1)
+        dve.tensor_scalar(T.diag[0:w, c0:c0 + w], T.ident[0:w, 0:w], T.negm[0:w, s:s + 1], None,
+                          mult).then_inc(S["d%d" % s], 1)
+        dve.wait_ge(S["c%d" % s], 5)
+        for u, r in enumerate(ranks[s]):
+            out = T.land[:, 0, :] if r == j else T.send[:, r ^ j, :]
+            dve.tensor_copy(out, ms[:, 0:2, QP * u:QP * u + QP]).then_inc(S["cp%d" % s], 1)
+
+    for s in range(1, NS):
+        rs = ranks[s]
+        masks, per = _split(common_mask(rs), len(rs))
+        g.wait_ge(S["cp%d" % s], len(rs))
+        g.remote_dma_fused([RemoteDMATransfer(dst_ids=[dst_id(r)], dma_engine_mask=masks[i], remote_sem=S["pa%d" % s],
+                                              src=T.send[:, r ^ j, :], dst=T.land[:, r ^ j, :]) for i, r in enumerate(rs)],
+                           local_sem=S.lsem)
+        lcount += per * len(rs)
+
+    def turn(s):
+        offs = STAGES[s]
+        if s == 0:
+            dve.wait_ge(S.cp0, 1)
+        else:
+            _, per = _split(common_mask(ranks[s]), len(offs))
+            dve.wait_ge(S["pa%d" % s], per * len(offs))
+        for o in offs:
+            dve.transpose(T.t1[:, o, :], T.land[:, o, :]).then_inc(S["t%d" % s], 1)
+
+    def combine(lo, hi, t, stages):
+        n = hi - lo
+        x, wp, mn = T["x" + t], T["wp" + t], T["mn" + t]
+        for s in stages:
+            dve.wait_ge(S["t%d" % s], len(STAGES[s]))
+            act.wait_ge(S["t%d" % s], len(STAGES[s]))
+        dve.tensor_reduce(mn[:, 0:1], T.t1[:, lo:hi, QP], axis=X, op=AluOpType.min).then_inc(S["mn" + t], 1)
+        act.wait_ge(S["mn" + t], 1)
+        act.activation(wp[:, 0:n, 0:QP - 1], T.t1[:, lo:hi, QP:2 * QP - 1], Exp, bias=mn[:, 0:1],
+                       scale=-1.0).then_inc(S["w" + t], 1)
+        dve.wait_ge(S["w" + t], 1)
+        dve.tensor_tensor(x[:, 0:n, 0:QP - 1], T.t1[:, lo:hi, 0:QP - 1], wp[:, 0:n, 0:QP - 1], mult).then_inc(S["x" + t], 1)
+        dve.tensor_tensor(x[:, 0:n, QP - 1:QP + 1], T.t1[:, lo:hi, QP - 1::QP], wp[:, 0:n, 0:2], mult).then_inc(S["x" + t], 1)
+        dve.wait_ge(S["x" + t], 2)
+        lvl = 0
+        while n > 1:
+            h = n // 2
+            dve.tensor_tensor(x[:, 0:h, :], x[:, 0:h, :], x[:, n - h:n, :], add).then_inc(S["u%d%s" % (lvl, t)], 1)
+            dve.wait_ge(S["u%d%s" % (lvl, t)], 1)
+            n -= h
+            lvl += 1
+        return x, mn
+
+    for s in range(PRE_STAGES):
+        turn(s)
+    x, mn = combine(0, NPRE, "p", range(PRE_STAGES))
+    dve.tensor_copy(T.t1[:, NPRE - 1, 0:QP], x[:, 0, 0:QP]).then_inc(S.sacc, 1)
+    dve.tensor_copy(T.t1[:, NPRE - 1, 2 * QP - 1:2 * QP], x[:, 0, QP:QP + 1]).then_inc(S.sacc, 1)
+    dve.tensor_scalar(T.t1[:, NPRE - 1, QP:2 * QP - 1], T.ones[:, 0:QP - 1], mn[:, 0:1], None, mult).then_inc(S.sacc, 1)
+    for s in range(PRE_STAGES, NS):
+        turn(s)
+    dve.wait_ge(S.sacc, 3)
+    act.wait_ge(S.sacc, 3)
+    x, mn = combine(NPRE - 1, 8, "f", range(PRE_STAGES, NS))
+    dve.reciprocal(T.rl[:, 0:1], x[:, 0, QP:QP + 1]).then_inc(S.srl, 1)
+    dve.wait_ge(S.srl, 1)
+    dve.tensor_scalar(T.yt[:, :], x[:, 0, 0:QP], T.rl[:, 0:1], None, mult).then_inc(S.syt, 1)
+
+    sp.wait_ge(S.syt, 1)
+    act.wait_ge(S.syt, 1)
+    for a in range(4):
+        q = sp if a % 2 == 0 else act
+        q.dma_start(T.y[:, QP * a:QP * a + QP], T.yt[QP * a:QP * a + QP, :]).then_inc(S.sy, 16)
+    sp.wait_ge(S.sy, 64)
+    g.wait_ge(S.lsem, lcount)

@@ -23,21 +23,23 @@ SCRATCH = {
     "land": ("sbuf", [128, 8, MW], "bfloat16"),
     "t1": ("sbuf", [128, 8, MW], "bfloat16"),
     "xp": ("sbuf", [128, 8, QP + 1], "float32"),
-    "xf": ("sbuf", [128, 8, QP + 1], "float32"),
+    "xf": ("sbuf", [128, 8, QP + 1], "bfloat16"),
     "mnp": ("sbuf", [128, 1], "float32"),
     "mnf": ("sbuf", [128, 1], "float32"),
+    "lsum": ("sbuf", [128, 1], "float32"),
     "rl": ("sbuf", [128, 1], "float32"),
     "yt": ("sbuf", [128, QP], "bfloat16"),
     "st": ("psum", [128, 512], "float32"),
-    "sp0": ("psum", [128, 512], "float32"),
-    "sp1": ("psum", [128, 512], "float32"),
+    "sp00": ("psum", [128, 512], "float32"),
+    "sp01": ("psum", [128, 512], "float32"),
+    "sp10": ("psum", [128, 512], "float32"),
+    "sp11": ("psum", [128, 512], "float32"),
     "ms0": ("psum", [128, 4, 128], "float32"),
     "ms1": ("psum", [128, 4, 128], "float32"),
-    "wpp": ("psum", [128, 16, QP], "float32"),
-    "wpf": ("psum", [128, 16, QP], "float32"),
+    "wps": ("psum", [128, 16, QP], "float32"),
 }
 
-SEMAPHORES = (["ldq", "ldk", "ldv", "sones", "sfill", "smask", "sident", "lsem", "sacc", "srl", "syt", "sy"]
+SEMAPHORES = (["ldq", "ldk", "ldv", "sones", "sfill", "smask", "sident", "lsem", "sacc", "sl", "srl", "sfin", "syt", "sy"]
               + ["%s%s" % (n, t) for t in "pf" for n in ("mn", "w", "x", "u0", "u1", "u2")]
               + ["%s%d" % (n, s) for s in range(NS)
                  for n in ("qa", "a", "r", "d", "ba", "bb", "ea", "eb", "c", "cp", "pa", "t")])
@@ -74,6 +76,12 @@ def rank_program(g, core, T, topo):
     ws = [QP * len(rs) for rs in ranks]
     myq = T.qall[:, QP * j:QP * j + QP]
 
+    def spb(b, s):
+        return T["sp%d%d" % (b, s % 2)]
+
+    def pcols(s, b):
+        return T.pbuf[:, 2 * c0s[s] + b * ws[s]:2 * c0s[s] + (b + 1) * ws[s]]
+
     sp.dma_start(myq, T.q[:, :]).then_inc(S.ldq, 16)
     act.dma_start(T.kbuf[:, :], T.k[:, :]).then_inc(S.ldk, 16)
     sp.dma_start(T.vbuf[:, :], T.v[:, :]).then_inc(S.ldv, 16)
@@ -98,11 +106,9 @@ def rank_program(g, core, T, topo):
                            local_sem=S.lsem)
         lcount += per
 
-    for s in range(NS):
+    def pe_a(s):
         w, c0 = ws[s], c0s[s]
-        ms = T["ms%d" % (s % 2)]
         qs = T.qall[:, c0:c0 + w]
-        dg = T.diag[0:w, c0:c0 + w]
         if s == 0:
             pe.wait_ge(S.ldq, 16)
             pe.wait_ge(S.ldk, 16)
@@ -111,36 +117,46 @@ def rank_program(g, core, T, topo):
             pe.wait_ge(S["qa%d" % s], per * len(ranks[s]))
         pe.matmul(T.st[0:w, 0:256], qs, T.kbuf[:, :], True, True).then_inc(S["a%d" % s], 1)
         for b, n in enumerate("ab"):
-            pe.matmul(T["sp%d" % b][:, 0:w], T.kbuf[:, 128 * b:128 * b + 128], qs, True, False).then_inc(S["b%s%d" % (n, s)], 1)
+            pe.matmul(spb(b, s)[:, 0:w], T.kbuf[:, 128 * b:128 * b + 128], qs, True, False).then_inc(S["b%s%d" % (n, s)], 1)
+
+    def pe_b(s):
+        w, c0 = ws[s], c0s[s]
+        dg = T.diag[0:w, c0:c0 + w]
         if s == 0:
             pe.wait_ge(S.sones, 1)
             pe.wait_ge(S.smask, 2)
         pe.wait_ge(S["d%d" % s], 1)
         for b, n in enumerate("ab"):
-            pe.matmul(T["sp%d" % b][:, 0:w], T.ones[0:w, :], dg, False, True).then_inc(S["b%s%d" % (n, s)], 1)
+            pe.matmul(spb(b, s)[:, 0:w], T.ones[0:w, :], dg, False, True).then_inc(S["b%s%d" % (n, s)], 1)
         if s >= 2:
             pe.wait_ge(S["cp%d" % (s - 2)], len(ranks[s - 2]))
-        pe.matmul(ms[:, 1, 0:w], T.onesa[0:w, :], dg, True, False).then_inc(S["c%d" % s], 1)
+        pe.matmul(T["ms%d" % (s % 2)][:, 1, 0:w], T.onesa[0:w, :], dg, True, False).then_inc(S["c%d" % s], 1)
+
+    def pe_c(s):
+        w = ws[s]
+        ms = T["ms%d" % (s % 2)]
         for b, n in enumerate("ab"):
             pe.wait_ge(S["e%s%d" % (n, s)], 1)
-            pe.matmul(ms[:, 1, 0:w], T.onesb[:, :], T.pbuf[:, 2 * c0 + b * w:2 * c0 + (b + 1) * w],
-                      False, b == 1).then_inc(S["c%d" % s], 1)
+            pe.matmul(ms[:, 1, 0:w], T.onesb[:, :], pcols(s, b), False, b == 1).then_inc(S["c%d" % s], 1)
         if s == 0:
             pe.wait_ge(S.ldv, 16)
         for b in range(2):
-            pe.matmul(ms[:, 0, 0:w], T.vbuf[:, 128 * b:128 * b + 128], T.pbuf[:, 2 * c0 + b * w:2 * c0 + (b + 1) * w],
-                      b == 0, b == 1).then_inc(S["c%d" % s], 1)
+            pe.matmul(ms[:, 0, 0:w], T.vbuf[:, 128 * b:128 * b + 128], pcols(s, b), b == 0, b == 1).then_inc(S["c%d" % s], 1)
+
+    pe_a(0)
+    for s in range(NS):
+        pe_b(s)
+        if s + 1 < NS:
+            pe_a(s + 1)
+        pe_c(s)
 
     for s in range(NS):
-        w, c0 = ws[s], c0s[s]
         for b, n in enumerate("ab"):
             act.wait_ge(S["b%s%d" % (n, s)], 2)
-            act.activation(T.pbuf[:, 2 * c0 + b * w:2 * c0 + (b + 1) * w], T["sp%d" % b][:, 0:w],
-                           Exp).then_inc(S["e%s%d" % (n, s)], 1)
+            act.activation(pcols(s, b), spb(b, s)[:, 0:ws[s]], Exp).then_inc(S["e%s%d" % (n, s)], 1)
 
-    for s in range(NS):
+    def dve_max(s):
         w, c0 = ws[s], c0s[s]
-        ms = T["ms%d" % (s % 2)]
         dve.wait_ge(S["a%d" % s], 1)
         dve.tensor_reduce(T.negm[0:w, s:s + 1], T.st[0:w, 0:256], axis=X, op=AluOpType.max,
                           negate=True).then_inc(S["r%d" % s], 1)
@@ -149,10 +165,15 @@ def rank_program(g, core, T, topo):
             dve.wait_ge(S.sident, 1)
         dve.tensor_scalar(T.diag[0:w, c0:c0 + w], T.ident[0:w, 0:w], T.negm[0:w, s:s + 1], None,
                           mult).then_inc(S["d%d" % s], 1)
+
+    dve_max(0)
+    for s in range(NS):
+        if s + 1 < NS:
+            dve_max(s + 1)
         dve.wait_ge(S["c%d" % s], 5)
         for u, r in enumerate(ranks[s]):
             out = T.land[:, 0, :] if r == j else T.send[:, r ^ j, :]
-            dve.tensor_copy(out, ms[:, 0:2, QP * u:QP * u + QP]).then_inc(S["cp%d" % s], 1)
+            dve.tensor_copy(out, T["ms%d" % (s % 2)][:, 0:2, QP * u:QP * u + QP]).then_inc(S["cp%d" % s], 1)
 
     for s in range(1, NS):
         rs = ranks[s]
@@ -173,32 +194,35 @@ def rank_program(g, core, T, topo):
         for o in offs:
             dve.transpose(T.t1[:, o, :], T.land[:, o, :]).then_inc(S["t%d" % s], 1)
 
-    def combine(lo, hi, t, stages):
+    def weigh(lo, hi, t, w0, stages):
         n = hi - lo
-        x, wp, mn = T["x" + t], T["wp" + t], T["mn" + t]
+        x, mn = T["x" + t], T["mn" + t]
+        wp = T.wps[:, w0:w0 + n, :]
         for s in stages:
             dve.wait_ge(S["t%d" % s], len(STAGES[s]))
             act.wait_ge(S["t%d" % s], len(STAGES[s]))
         dve.tensor_reduce(mn[:, 0:1], T.t1[:, lo:hi, QP], axis=X, op=AluOpType.min).then_inc(S["mn" + t], 1)
         act.wait_ge(S["mn" + t], 1)
-        act.activation(wp[:, 0:n, 0:QP - 1], T.t1[:, lo:hi, QP:2 * QP - 1], Exp, bias=mn[:, 0:1],
+        act.activation(T.wps[:, w0:w0 + n, 0:QP - 1], T.t1[:, lo:hi, QP:2 * QP - 1], Exp, bias=mn[:, 0:1],
                        scale=-1.0).then_inc(S["w" + t], 1)
         dve.wait_ge(S["w" + t], 1)
-        dve.tensor_tensor(x[:, 0:n, 0:QP - 1], T.t1[:, lo:hi, 0:QP - 1], wp[:, 0:n, 0:QP - 1], mult).then_inc(S["x" + t], 1)
-        dve.tensor_tensor(x[:, 0:n, QP - 1:QP + 1], T.t1[:, lo:hi, QP - 1::QP], wp[:, 0:n, 0:2], mult).then_inc(S["x" + t], 1)
-        dve.wait_ge(S["x" + t], 2)
-        lvl = 0
-        while n > 1:
-            h = n // 2
-            dve.tensor_tensor(x[:, 0:h, :], x[:, 0:h, :], x[:, n - h:n, :], add).then_inc(S["u%d%s" % (lvl, t)], 1)
-            dve.wait_ge(S["u%d%s" % (lvl, t)], 1)
-            n -= h
-            lvl += 1
-        return x, mn
+        dve.tensor_tensor(x[:, 0:n, QP - 1:QP + 1], T.t1[:, lo:hi, QP - 1::QP], T.wps[:, w0:w0 + n, 0:2],
+                          mult).then_inc(S["x" + t], 1)
+        dve.tensor_tensor(x[:, 0:n, 0:QP - 1], T.t1[:, lo:hi, 0:QP - 1], T.wps[:, w0:w0 + n, 0:QP - 1],
+                          mult).then_inc(S["x" + t], 1)
+        return x, mn, n
 
     for s in range(PRE_STAGES):
         turn(s)
-    x, mn = combine(0, NPRE, "p", range(PRE_STAGES))
+    x, mn, n = weigh(0, NPRE, "p", 0, range(PRE_STAGES))
+    dve.wait_ge(S.xp, 2)
+    lvl = 0
+    while n > 1:
+        h = n // 2
+        dve.tensor_tensor(x[:, 0:h, :], x[:, 0:h, :], x[:, n - h:n, :], add).then_inc(S["u%dp" % lvl], 1)
+        dve.wait_ge(S["u%dp" % lvl], 1)
+        n -= h
+        lvl += 1
     dve.tensor_copy(T.t1[:, NPRE - 1, 0:QP], x[:, 0, 0:QP]).then_inc(S.sacc, 1)
     dve.tensor_copy(T.t1[:, NPRE - 1, 2 * QP - 1:2 * QP], x[:, 0, QP:QP + 1]).then_inc(S.sacc, 1)
     dve.tensor_scalar(T.t1[:, NPRE - 1, QP:2 * QP - 1], T.ones[:, 0:QP - 1], mn[:, 0:1], None, mult).then_inc(S.sacc, 1)
@@ -206,10 +230,17 @@ def rank_program(g, core, T, topo):
         turn(s)
     dve.wait_ge(S.sacc, 3)
     act.wait_ge(S.sacc, 3)
-    x, mn = combine(NPRE - 1, 8, "f", range(PRE_STAGES, NS))
-    dve.reciprocal(T.rl[:, 0:1], x[:, 0, QP:QP + 1]).then_inc(S.srl, 1)
+    x, mn, n = weigh(NPRE - 1, 8, "f", 8, range(PRE_STAGES, NS))
+    pe.wait_ge(S.xf, 2)
+    for i in range(n):
+        pe.matmul(T.st[:, 0:QP], T.ident[:, :], x[:, i, 0:QP], i == 0, i == n - 1).then_inc(S.sfin, 1)
+    dve.wait_ge(S.xf, 2)
+    dve.tensor_reduce(T.lsum[:, 0:1], x[:, 0:n, QP], axis=X, op=add).then_inc(S.sl, 1)
+    dve.wait_ge(S.sl, 1)
+    dve.reciprocal(T.rl[:, 0:1], T.lsum[:, 0:1]).then_inc(S.srl, 1)
     dve.wait_ge(S.srl, 1)
-    dve.tensor_scalar(T.yt[:, :], x[:, 0, 0:QP], T.rl[:, 0:1], None, mult).then_inc(S.syt, 1)
+    dve.wait_ge(S.sfin, n)
+    dve.tensor_scalar(T.yt[:, :], T.st[:, 0:QP], T.rl[:, 0:1], None, mult).then_inc(S.syt, 1)
 
     sp.wait_ge(S.syt, 1)
     act.wait_ge(S.syt, 1)

@@ -3,10 +3,10 @@ from concourse.mybir import AluOpType, AxisListType, ActivationFunctionType
 
 QP = 32
 MW = 2 * QP
-STAGES = [(0,), (1,), (2, 3), (4, 5), (6, 7)]
-NS = len(STAGES)
+SIZES = [1, 1, 2, 2, 2]
+NS = len(SIZES)
 PRE_STAGES = 3
-NPRE = sum(len(o) for o in STAGES[:PRE_STAGES])
+NPRE = sum(SIZES[:PRE_STAGES])
 
 SCRATCH = {
     "qall": ("sbuf", [128, 256], "bfloat16"),
@@ -22,25 +22,25 @@ SCRATCH = {
     "send": ("sbuf", [128, 8, MW], "bfloat16"),
     "land": ("sbuf", [128, 8, MW], "bfloat16"),
     "t1": ("sbuf", [128, 8, MW], "bfloat16"),
-    "xp": ("sbuf", [128, 8, QP + 1], "float32"),
+    "xp": ("sbuf", [128, 8, QP + 1], "bfloat16"),
     "xf": ("sbuf", [128, 8, QP + 1], "bfloat16"),
     "mnp": ("sbuf", [128, 1], "float32"),
     "mnf": ("sbuf", [128, 1], "float32"),
     "lsum": ("sbuf", [128, 1], "float32"),
     "rl": ("sbuf", [128, 1], "float32"),
     "yt": ("sbuf", [128, QP], "bfloat16"),
-    "st": ("psum", [128, 512], "float32"),
+    "st0": ("psum", [128, 512], "float32"),
+    "st1": ("psum", [128, 512], "float32"),
     "sp00": ("psum", [128, 512], "float32"),
     "sp01": ("psum", [128, 512], "float32"),
     "sp10": ("psum", [128, 512], "float32"),
     "sp11": ("psum", [128, 512], "float32"),
-    "ms0": ("psum", [128, 4, 128], "float32"),
-    "ms1": ("psum", [128, 4, 128], "float32"),
-    "wps": ("psum", [128, 16, QP], "float32"),
+    "ms0": ("psum", [128, 8, MW], "float32"),
+    "ms1": ("psum", [128, 8, MW], "float32"),
 }
 
 SEMAPHORES = (["ldq", "ldk", "ldv", "sones", "sfill", "smask", "sident", "lsem", "sacc", "sl", "srl", "sfin", "syt", "sy"]
-              + ["%s%s" % (n, t) for t in "pf" for n in ("mn", "w", "x", "u0", "u1", "u2")]
+              + ["%s%s" % (n, t) for t in "pf" for n in ("mn", "w", "x", "u0")]
               + ["%s%d" % (n, s) for s in range(NS)
                  for n in ("qa", "a", "r", "d", "ba", "bb", "ea", "eb", "c", "cp", "pa", "t")])
 
@@ -49,6 +49,16 @@ def _split(mask, n):
     bits = [b for b in range(mask.bit_length()) if (mask >> b) & 1]
     per = len(bits) // n
     return [sum(1 << b for b in bits[i * per:(i + 1) * per]) for i in range(n)], per
+
+
+def _order(T, topo):
+    c0 = T.cores[0]
+
+    def far(o):
+        c = T.cores[o]
+        return 0 if topo.mates(c0, c) else (1 if topo.same_plane(c0, c) else 2)
+
+    return [0] + sorted(range(1, len(T.cores)), key=lambda o: (far(o) != 0, -far(o), o))
 
 
 def rank_program(g, core, T, topo):
@@ -71,10 +81,16 @@ def rank_program(g, core, T, topo):
             m &= topo.mask(core, T.cores[r])
         return m
 
-    ranks = [sorted(j ^ o for o in offs) for offs in STAGES]
-    c0s = [QP * rs[0] for rs in ranks]
-    ws = [QP * len(rs) for rs in ranks]
-    myq = T.qall[:, QP * j:QP * j + QP]
+    order = _order(T, topo)
+    p0s = [sum(SIZES[:s]) for s in range(NS)]
+    ranks = [[j ^ order[p0s[s] + i] for i in range(SIZES[s])] for s in range(NS)]
+    c0s = [QP * p for p in p0s]
+    ws = [QP * n for n in SIZES]
+
+    def qslot(p):
+        return T.qall[:, QP * p:QP * p + QP]
+
+    myq = qslot(0)
 
     def spb(b, s):
         return T["sp%d%d" % (b, s % 2)]
@@ -102,24 +118,28 @@ def rank_program(g, core, T, topo):
         m = common_mask(rs)
         _, per = _split(m, 1)
         g.remote_dma_fused([RemoteDMATransfer(dst_ids=[dst_id(r) for r in rs], dma_engine_mask=m,
-                                              remote_sem=S["qa%d" % s], srcs=[myq], dsts=[myq for r in rs])],
+                                              remote_sem=S["qa%d" % s], srcs=[myq],
+                                              dsts=[qslot(p0s[s] + i) for i in range(len(rs))])],
                            local_sem=S.lsem)
         lcount += per
 
-    def pe_a(s):
+    def pe_st(s):
         w, c0 = ws[s], c0s[s]
-        qs = T.qall[:, c0:c0 + w]
         if s == 0:
             pe.wait_ge(S.ldq, 16)
             pe.wait_ge(S.ldk, 16)
         else:
             _, per = _split(common_mask(ranks[s]), 1)
             pe.wait_ge(S["qa%d" % s], per * len(ranks[s]))
-        pe.matmul(T.st[0:w, 0:256], qs, T.kbuf[:, :], True, True).then_inc(S["a%d" % s], 1)
-        for b, n in enumerate("ab"):
-            pe.matmul(spb(b, s)[:, 0:w], T.kbuf[:, 128 * b:128 * b + 128], qs, True, False).then_inc(S["b%s%d" % (n, s)], 1)
+        pe.matmul(T["st%d" % (s % 2)][0:w, 0:256], T.qall[:, c0:c0 + w], T.kbuf[:, :], True, True).then_inc(S["a%d" % s], 1)
 
-    def pe_b(s):
+    def pe_op(s):
+        w, c0 = ws[s], c0s[s]
+        for b, n in enumerate("ab"):
+            pe.matmul(spb(b, s)[:, 0:w], T.kbuf[:, 128 * b:128 * b + 128], T.qall[:, c0:c0 + w], True,
+                      False).then_inc(S["b%s%d" % (n, s)], 1)
+
+    def pe_sh(s):
         w, c0 = ws[s], c0s[s]
         dg = T.diag[0:w, c0:c0 + w]
         if s == 0:
@@ -132,7 +152,7 @@ def rank_program(g, core, T, topo):
             pe.wait_ge(S["cp%d" % (s - 2)], len(ranks[s - 2]))
         pe.matmul(T["ms%d" % (s % 2)][:, 1, 0:w], T.onesa[0:w, :], dg, True, False).then_inc(S["c%d" % s], 1)
 
-    def pe_c(s):
+    def pe_pv(s):
         w = ws[s]
         ms = T["ms%d" % (s % 2)]
         for b, n in enumerate("ab"):
@@ -143,12 +163,17 @@ def rank_program(g, core, T, topo):
         for b in range(2):
             pe.matmul(ms[:, 0, 0:w], T.vbuf[:, 128 * b:128 * b + 128], pcols(s, b), b == 0, b == 1).then_inc(S["c%d" % s], 1)
 
-    pe_a(0)
+    pe_st(0)
+    pe_op(0)
     for s in range(NS):
-        pe_b(s)
+        pe_sh(s)
+        if s == 0:
+            pe_st(1)
         if s + 1 < NS:
-            pe_a(s + 1)
-        pe_c(s)
+            pe_op(s + 1)
+        if s + 2 < NS:
+            pe_st(s + 2)
+        pe_pv(s)
 
     for s in range(NS):
         for b, n in enumerate("ab"):
@@ -158,7 +183,7 @@ def rank_program(g, core, T, topo):
     def dve_max(s):
         w, c0 = ws[s], c0s[s]
         dve.wait_ge(S["a%d" % s], 1)
-        dve.tensor_reduce(T.negm[0:w, s:s + 1], T.st[0:w, 0:256], axis=X, op=AluOpType.max,
+        dve.tensor_reduce(T.negm[0:w, s:s + 1], T["st%d" % (s % 2)][0:w, 0:256], axis=X, op=AluOpType.max,
                           negate=True).then_inc(S["r%d" % s], 1)
         dve.wait_ge(S["r%d" % s], 1)
         if s == 0:
@@ -167,12 +192,13 @@ def rank_program(g, core, T, topo):
                           mult).then_inc(S["d%d" % s], 1)
 
     dve_max(0)
+    dve_max(1)
     for s in range(NS):
-        if s + 1 < NS:
-            dve_max(s + 1)
+        if s + 2 < NS:
+            dve_max(s + 2)
         dve.wait_ge(S["c%d" % s], 5)
-        for u, r in enumerate(ranks[s]):
-            out = T.land[:, 0, :] if r == j else T.send[:, r ^ j, :]
+        for u in range(SIZES[s]):
+            out = T.land[:, 0, :] if s == 0 else T.send[:, p0s[s] + u, :]
             dve.tensor_copy(out, T["ms%d" % (s % 2)][:, 0:2, QP * u:QP * u + QP]).then_inc(S["cp%d" % s], 1)
 
     for s in range(1, NS):
@@ -180,67 +206,65 @@ def rank_program(g, core, T, topo):
         masks, per = _split(common_mask(rs), len(rs))
         g.wait_ge(S["cp%d" % s], len(rs))
         g.remote_dma_fused([RemoteDMATransfer(dst_ids=[dst_id(r)], dma_engine_mask=masks[i], remote_sem=S["pa%d" % s],
-                                              src=T.send[:, r ^ j, :], dst=T.land[:, r ^ j, :]) for i, r in enumerate(rs)],
-                           local_sem=S.lsem)
+                                              src=T.send[:, p0s[s] + i, :], dst=T.land[:, p0s[s] + i, :])
+                            for i, r in enumerate(rs)], local_sem=S.lsem)
         lcount += per * len(rs)
 
     def turn(s):
-        offs = STAGES[s]
         if s == 0:
             dve.wait_ge(S.cp0, 1)
         else:
-            _, per = _split(common_mask(ranks[s]), len(offs))
-            dve.wait_ge(S["pa%d" % s], per * len(offs))
-        for o in offs:
-            dve.transpose(T.t1[:, o, :], T.land[:, o, :]).then_inc(S["t%d" % s], 1)
+            _, per = _split(common_mask(ranks[s]), SIZES[s])
+            dve.wait_ge(S["pa%d" % s], per * SIZES[s])
+        for p in range(p0s[s], p0s[s] + SIZES[s]):
+            dve.transpose(T.t1[:, p, :], T.land[:, p, :]).then_inc(S["t%d" % s], 1)
 
-    def weigh(lo, hi, t, w0, stages):
+    def weigh(lo, hi, t, wp, stages):
         n = hi - lo
         x, mn = T["x" + t], T["mn" + t]
-        wp = T.wps[:, w0:w0 + n, :]
         for s in stages:
-            dve.wait_ge(S["t%d" % s], len(STAGES[s]))
-            act.wait_ge(S["t%d" % s], len(STAGES[s]))
+            dve.wait_ge(S["t%d" % s], SIZES[s])
+            act.wait_ge(S["t%d" % s], SIZES[s])
         dve.tensor_reduce(mn[:, 0:1], T.t1[:, lo:hi, QP], axis=X, op=AluOpType.min).then_inc(S["mn" + t], 1)
         act.wait_ge(S["mn" + t], 1)
-        act.activation(T.wps[:, w0:w0 + n, 0:QP - 1], T.t1[:, lo:hi, QP:2 * QP - 1], Exp, bias=mn[:, 0:1],
+        act.activation(wp[:, 0:n, 0:QP - 1], T.t1[:, lo:hi, QP:2 * QP - 1], Exp, bias=mn[:, 0:1],
                        scale=-1.0).then_inc(S["w" + t], 1)
         dve.wait_ge(S["w" + t], 1)
-        dve.tensor_tensor(x[:, 0:n, QP - 1:QP + 1], T.t1[:, lo:hi, QP - 1::QP], T.wps[:, w0:w0 + n, 0:2],
+        dve.tensor_tensor(x[:, 0:n, QP - 1:QP + 1], T.t1[:, lo:hi, QP - 1::QP], wp[:, 0:n, 0:2],
                           mult).then_inc(S["x" + t], 1)
-        dve.tensor_tensor(x[:, 0:n, 0:QP - 1], T.t1[:, lo:hi, 0:QP - 1], T.wps[:, w0:w0 + n, 0:QP - 1],
+        dve.tensor_tensor(x[:, 0:n, 0:QP - 1], T.t1[:, lo:hi, 0:QP - 1], wp[:, 0:n, 0:QP - 1],
                           mult).then_inc(S["x" + t], 1)
         return x, mn, n
 
+    for s in (NS - 2, NS - 1):
+        act.wait_ge(S["cp%d" % s], SIZES[s])
     for s in range(PRE_STAGES):
         turn(s)
-    x, mn, n = weigh(0, NPRE, "p", 0, range(PRE_STAGES))
-    dve.wait_ge(S.xp, 2)
-    lvl = 0
-    while n > 1:
-        h = n // 2
-        dve.tensor_tensor(x[:, 0:h, :], x[:, 0:h, :], x[:, n - h:n, :], add).then_inc(S["u%dp" % lvl], 1)
-        dve.wait_ge(S["u%dp" % lvl], 1)
-        n -= h
-        lvl += 1
-    dve.tensor_copy(T.t1[:, NPRE - 1, 0:QP], x[:, 0, 0:QP]).then_inc(S.sacc, 1)
-    dve.tensor_copy(T.t1[:, NPRE - 1, 2 * QP - 1:2 * QP], x[:, 0, QP:QP + 1]).then_inc(S.sacc, 1)
+    x, mn, n = weigh(0, NPRE, "p", T["ms%d" % ((NS - 2) % 2)], range(PRE_STAGES))
     dve.tensor_scalar(T.t1[:, NPRE - 1, QP:2 * QP - 1], T.ones[:, 0:QP - 1], mn[:, 0:1], None, mult).then_inc(S.sacc, 1)
-    for s in range(PRE_STAGES, NS):
+    pe.wait_ge(S.xp, 2)
+    for i in range(n):
+        pe.matmul(T.st1[:, 0:QP + 1], T.ident[:, :], x[:, i, :], i == 0, i == n - 1).then_inc(S.u0p, 1)
+    for s in range(PRE_STAGES, NS - 1):
         turn(s)
+    dve.wait_ge(S.xp, 2)
+    dve.wait_ge(S.u0p, n)
+    dve.tensor_copy(T.t1[:, NPRE - 1, 0:QP], T.st1[:, 0:QP]).then_inc(S.sacc, 1)
+    dve.tensor_copy(T.t1[:, NPRE - 1, 2 * QP - 1:2 * QP], T.st1[:, QP:QP + 1]).then_inc(S.sacc, 1)
+    turn(NS - 1)
     dve.wait_ge(S.sacc, 3)
     act.wait_ge(S.sacc, 3)
-    x, mn, n = weigh(NPRE - 1, 8, "f", 8, range(PRE_STAGES, NS))
+    x, mn, n = weigh(NPRE - 1, 8, "f", T["ms%d" % ((NS - 1) % 2)], range(PRE_STAGES, NS))
     pe.wait_ge(S.xf, 2)
     for i in range(n):
-        pe.matmul(T.st[:, 0:QP], T.ident[:, :], x[:, i, 0:QP], i == 0, i == n - 1).then_inc(S.sfin, 1)
+        pe.matmul(T.st0[:, 0:QP], T.ident[:, :], x[:, i, 0:QP], i == 0, i == n - 1).then_inc(S.sfin, 1)
     dve.wait_ge(S.xf, 2)
     dve.tensor_reduce(T.lsum[:, 0:1], x[:, 0:n, QP], axis=X, op=add).then_inc(S.sl, 1)
     dve.wait_ge(S.sl, 1)
     dve.reciprocal(T.rl[:, 0:1], T.lsum[:, 0:1]).then_inc(S.srl, 1)
     dve.wait_ge(S.srl, 1)
     dve.wait_ge(S.sfin, n)
-    dve.tensor_scalar(T.yt[:, :], T.st[:, 0:QP], T.rl[:, 0:1], None, mult).then_inc(S.syt, 1)
+    dve.tensor_scalar(T.yt[:, :], T.st0[:, 0:QP], T.rl[:, 0:1], None, mult).then_inc(S.syt, 1)
 
     sp.wait_ge(S.syt, 1)
     act.wait_ge(S.syt, 1)

from concourse.bass import DstId, RemoteDMATransfer
from concourse.mybir import AluOpType, AxisListType, ActivationFunctionType

QP = 32
MW = 2 * QP
SIZES = [1, 1, 2, 2, 2]
NS = len(SIZES)
PRE_STAGES = 3
NPRE = sum(SIZES[:PRE_STAGES])

SCRATCH = {
    "qall": ("sbuf", [128, 256], "bfloat16"),
    "kbuf": ("sbuf", [128, 256], "bfloat16"),
    "vbuf": ("sbuf", [128, 256], "bfloat16"),
    "ones": ("sbuf", [128, 128], "bfloat16"),
    "onesa": ("sbuf", [128, 128], "bfloat16"),
    "onesb": ("sbuf", [128, 128], "bfloat16"),
    "ident": ("sbuf", [128, 128], "bfloat16"),
    "negm": ("sbuf", [128, 8], "bfloat16"),
    "diag": ("sbuf", [128, 256], "bfloat16"),
    "pbuf": ("sbuf", [128, 512], "bfloat16"),
    "send": ("sbuf", [128, 8, MW], "bfloat16"),
    "land": ("sbuf", [128, 8, MW], "bfloat16"),
    "t1": ("sbuf", [128, 8, MW], "bfloat16"),
    "xp": ("sbuf", [128, 8, QP + 1], "bfloat16"),
    "xf": ("sbuf", [128, 8, QP + 1], "bfloat16"),
    "mnp": ("sbuf", [128, 1], "float32"),
    "mnf": ("sbuf", [128, 1], "float32"),
    "lsum": ("sbuf", [128, 1], "float32"),
    "rl": ("sbuf", [128, 1], "float32"),
    "yt": ("sbuf", [128, QP], "bfloat16"),
    "st0": ("psum", [128, 512], "float32"),
    "st1": ("psum", [128, 512], "float32"),
    "sp00": ("psum", [128, 512], "float32"),
    "sp01": ("psum", [128, 512], "float32"),
    "sp10": ("psum", [128, 512], "float32"),
    "sp11": ("psum", [128, 512], "float32"),
    "ms0": ("psum", [128, 8, MW], "float32"),
    "ms1": ("psum", [128, 8, MW], "float32"),
}

SEMAPHORES = (["ldq", "ldk", "ldv", "sones", "sfill", "smask", "sident", "lsem", "sacc", "sl", "srl", "sfin", "syt", "sy"]
              + ["%s%s" % (n, t) for t in "pf" for n in ("mn", "w", "x", "u0")]
              + ["%s%d" % (n, s) for s in range(NS)
                 for n in ("qa", "a", "r", "d", "ba", "bb", "ea", "eb", "c", "cp", "pa", "t")])


def _split(mask, n):
    bits = [b for b in range(mask.bit_length()) if (mask >> b) & 1]
    per = len(bits) // n
    return [sum(1 << b for b in bits[i * per:(i + 1) * per]) for i in range(n)], per


def _order(T, topo):
    c0 = T.cores[0]

    def far(o):
        c = T.cores[o]
        return 0 if topo.mates(c0, c) else (1 if topo.same_plane(c0, c) else 2)

    return [0] + sorted(range(1, len(T.cores)), key=lambda o: (far(o) != 0, -far(o), o))


def rank_program(g, core, T, topo):
    j = T.rank_of(core)
    if j is None:
        return
    pe, dve, act, sp = g.tensor, g.vector, g.scalar, g.sync
    S = T.sem
    Exp = ActivationFunctionType.Exp
    X = AxisListType.X
    mult, add = AluOpType.mult, AluOpType.add

    def dst_id(r):
        rid, pid = topo.addr(T.cores[r], core)
        return DstId(rid=rid, pnc=pid)

    def common_mask(rs):
        m = topo.mask(core, T.cores[rs[0]])
        for r in rs[1:]:
            m &= topo.mask(core, T.cores[r])
        return m

    order = _order(T, topo)
    p0s = [sum(SIZES[:s]) for s in range(NS)]
    ranks = [[j ^ order[p0s[s] + i] for i in range(SIZES[s])] for s in range(NS)]
    c0s = [QP * p for p in p0s]
    ws = [QP * n for n in SIZES]

    def qslot(p):
        return T.qall[:, QP * p:QP * p + QP]

    myq = qslot(0)

    def spb(b, s):
        return T["sp%d%d" % (b, s % 2)]

    def pcols(s, b):
        return T.pbuf[:, 2 * c0s[s] + b * ws[s]:2 * c0s[s] + (b + 1) * ws[s]]

    sp.dma_start(myq, T.q[:, :]).then_inc(S.ldq, 16)
    act.dma_start(T.kbuf[:, :], T.k[:, :]).then_inc(S.ldk, 16)
    sp.dma_start(T.vbuf[:, :], T.v[:, :]).then_inc(S.ldv, 16)

    dve.memset(T.ones[:, :], 1.0).then_inc(S.sones, 1)
    dve.memset(T.onesa[:, :], 1.0).then_inc(S.sfill, 1)
    dve.memset(T.onesb[:, :], 0.0).then_inc(S.sfill, 1)
    dve.wait_ge(S.sfill, 2)
    dve.memset(T.onesa[:, QP - 1::QP], 0.0).then_inc(S.smask, 1)
    dve.memset(T.onesb[:, QP - 1::QP], 1.0).then_inc(S.smask, 1)
    g.wait_ge(S.sones, 1)
    g.affine_select(T.ident[:, :], T.ones[:, :], [[-1, 128]], AluOpType.is_equal, 0.0, 0, 1).then_inc(S.sident, 1)

    lcount = 0
    g.wait_ge(S.ldq, 16)
    for s in range(1, NS):
        rs = ranks[s]
        m = common_mask(rs)
        _, per = _split(m, 1)
        g.remote_dma_fused([RemoteDMATransfer(dst_ids=[dst_id(r) for r in rs], dma_engine_mask=m,
                                              remote_sem=S["qa%d" % s], srcs=[myq],
                                              dsts=[qslot(p0s[s] + i) for i in range(len(rs))])],
                           local_sem=S.lsem)
        lcount += per

    def pe_st(s):
        w, c0 = ws[s], c0s[s]
        if s == 0:
            pe.wait_ge(S.ldq, 16)
            pe.wait_ge(S.ldk, 16)
        else:
            _, per = _split(common_mask(ranks[s]), 1)
            pe.wait_ge(S["qa%d" % s], per * len(ranks[s]))
        pe.matmul(T["st%d" % (s % 2)][0:w, 0:256], T.qall[:, c0:c0 + w], T.kbuf[:, :], True, True).then_inc(S["a%d" % s], 1)

    def pe_op(s):
        w, c0 = ws[s], c0s[s]
        for b, n in enumerate("ab"):
            pe.matmul(spb(b, s)[:, 0:w], T.kbuf[:, 128 * b:128 * b + 128], T.qall[:, c0:c0 + w], True,
                      False).then_inc(S["b%s%d" % (n, s)], 1)

    def pe_sh(s):
        w, c0 = ws[s], c0s[s]
        dg = T.diag[0:w, c0:c0 + w]
        if s == 0:
            pe.wait_ge(S.sones, 1)
            pe.wait_ge(S.smask, 2)
        pe.wait_ge(S["d%d" % s], 1)
        for b, n in enumerate("ab"):
            pe.matmul(spb(b, s)[:, 0:w], T.ones[0:w, :], dg, False, True).then_inc(S["b%s%d" % (n, s)], 1)
        if s >= 2:
            pe.wait_ge(S["cp%d" % (s - 2)], len(ranks[s - 2]))
        pe.matmul(T["ms%d" % (s % 2)][:, 1, 0:w], T.onesa[0:w, :], dg, True, False).then_inc(S["c%d" % s], 1)

    def pe_pv(s):
        w = ws[s]
        ms = T["ms%d" % (s % 2)]
        for b, n in enumerate("ab"):
            pe.wait_ge(S["e%s%d" % (n, s)], 1)
            pe.matmul(ms[:, 1, 0:w], T.onesb[:, :], pcols(s, b), False, b == 1).then_inc(S["c%d" % s], 1)
        if s == 0:
            pe.wait_ge(S.ldv, 16)
        for b in range(2):
            pe.matmul(ms[:, 0, 0:w], T.vbuf[:, 128 * b:128 * b + 128], pcols(s, b), b == 0, b == 1).then_inc(S["c%d" % s], 1)

    pe_st(0)
    pe_op(0)
    for s in range(NS):
        pe_sh(s)
        if s == 0:
            pe_st(1)
        if s + 1 < NS:
            pe_op(s + 1)
        if s + 2 < NS:
            pe_st(s + 2)
        pe_pv(s)

    for s in range(NS):
        for b, n in enumerate("ab"):
            act.wait_ge(S["b%s%d" % (n, s)], 2)
            act.activation(pcols(s, b), spb(b, s)[:, 0:ws[s]], Exp).then_inc(S["e%s%d" % (n, s)], 1)

    def dve_max(s):
        w, c0 = ws[s], c0s[s]
        dve.wait_ge(S["a%d" % s], 1)
        dve.tensor_reduce(T.negm[0:w, s:s + 1], T["st%d" % (s % 2)][0:w, 0:256], axis=X, op=AluOpType.max,
                          negate=True).then_inc(S["r%d" % s], 1)
        dve.wait_ge(S["r%d" % s], 1)
        if s == 0:
            dve.wait_ge(S.sident, 1)
        dve.tensor_scalar(T.diag[0:w, c0:c0 + w], T.ident[0:w, 0:w], T.negm[0:w, s:s + 1], None,
                          mult).then_inc(S["d%d" % s], 1)

    dve_max(0)
    dve_max(1)
    for s in range(NS):
        if s + 2 < NS:
            dve_max(s + 2)
        dve.wait_ge(S["c%d" % s], 5)
        for u in range(SIZES[s]):
            out = T.land[:, 0, :] if s == 0 else T.send[:, p0s[s] + u, :]
            dve.tensor_copy(out, T["ms%d" % (s % 2)][:, 0:2, QP * u:QP * u + QP]).then_inc(S["cp%d" % s], 1)

    for s in range(1, NS):
        rs = ranks[s]
        masks, per = _split(common_mask(rs), len(rs))
        g.wait_ge(S["cp%d" % s], len(rs))
        g.remote_dma_fused([RemoteDMATransfer(dst_ids=[dst_id(r)], dma_engine_mask=masks[i], remote_sem=S["pa%d" % s],
                                              src=T.send[:, p0s[s] + i, :], dst=T.land[:, p0s[s] + i, :])
                            for i, r in enumerate(rs)], local_sem=S.lsem)
        lcount += per * len(rs)

    def turn(s):
        if s == 0:
            dve.wait_ge(S.cp0, 1)
        else:
            _, per = _split(common_mask(ranks[s]), SIZES[s])
            dve.wait_ge(S["pa%d" % s], per * SIZES[s])
        for p in range(p0s[s], p0s[s] + SIZES[s]):
            dve.transpose(T.t1[:, p, :], T.land[:, p, :]).then_inc(S["t%d" % s], 1)

    def weigh(lo, hi, t, wp, stages):
        n = hi - lo
        x, mn = T["x" + t], T["mn" + t]
        for s in stages:
            dve.wait_ge(S["t%d" % s], SIZES[s])
            act.wait_ge(S["t%d" % s], SIZES[s])
        dve.tensor_reduce(mn[:, 0:1], T.t1[:, lo:hi, QP], axis=X, op=AluOpType.min).then_inc(S["mn" + t], 1)
        act.wait_ge(S["mn" + t], 1)
        act.activation(wp[:, 0:n, 0:QP - 1], T.t1[:, lo:hi, QP:2 * QP - 1], Exp, bias=mn[:, 0:1],
                       scale=-1.0).then_inc(S["w" + t], 1)
        dve.wait_ge(S["w" + t], 1)
        dve.tensor_tensor(x[:, 0:n, QP - 1:QP + 1], T.t1[:, lo:hi, QP - 1::QP], wp[:, 0:n, 0:2],
                          mult).then_inc(S["x" + t], 1)
        dve.tensor_tensor(x[:, 0:n, 0:QP - 1], T.t1[:, lo:hi, 0:QP - 1], wp[:, 0:n, 0:QP - 1],
                          mult).then_inc(S["x" + t], 1)
        return x, mn, n

    for s in (NS - 2, NS - 1):
        act.wait_ge(S["cp%d" % s], SIZES[s])
    for s in range(PRE_STAGES):
        turn(s)
    x, mn, n = weigh(0, NPRE, "p", T["ms%d" % ((NS - 2) % 2)], range(PRE_STAGES))
    dve.tensor_scalar(T.t1[:, NPRE - 1, QP:2 * QP - 1], T.ones[:, 0:QP - 1], mn[:, 0:1], None, mult).then_inc(S.sacc, 1)
    pe.wait_ge(S.xp, 2)
    for i in range(n):
        pe.matmul(T.st1[:, 0:QP + 1], T.ident[:, :], x[:, i, :], i == 0, i == n - 1).then_inc(S.u0p, 1)
    for s in range(PRE_STAGES, NS - 1):
        turn(s)
    dve.wait_ge(S.xp, 2)
    dve.wait_ge(S.u0p, n)
    dve.tensor_copy(T.t1[:, NPRE - 1, 0:QP], T.st1[:, 0:QP]).then_inc(S.sacc, 1)
    dve.tensor_copy(T.t1[:, NPRE - 1, 2 * QP - 1:2 * QP], T.st1[:, QP:QP + 1]).then_inc(S.sacc, 1)
    turn(NS - 1)
    dve.wait_ge(S.sacc, 3)
    act.wait_ge(S.sacc, 3)
    x, mn, n = weigh(NPRE - 1, 8, "f", T["ms%d" % ((NS - 1) % 2)], range(PRE_STAGES, NS))
    pe.wait_ge(S.xf, 2)
    for i in range(n):
        pe.matmul(T.st0[:, 0:QP], T.ident[:, :], x[:, i, 0:QP], i == 0, i == n - 1).then_inc(S.sfin, 1)
    dve.wait_ge(S.xf, 2)
    dve.tensor_reduce(T.lsum[:, 0:1], x[:, 0:n, QP], axis=X, op=add).then_inc(S.sl, 1)
    dve.wait_ge(S.sl, 1)
    dve.reciprocal(T.rl[:, 0:1], T.lsum[:, 0:1]).then_inc(S.srl, 1)
    dve.wait_ge(S.srl, 1)
    dve.wait_ge(S.sfin, n)
    dve.tensor_scalar(T.yt[:, :], T.st0[:, 0:QP], T.rl[:, 0:1], None, mult).then_inc(S.syt, 1)

    sp.wait_ge(S.syt, 1)
    act.wait_ge(S.syt, 1)
    for a in range(4):
        q = sp if a % 2 == 0 else act
        q.dma_start(T.y[:, QP * a:QP * a + QP], T.yt[QP * a:QP * a + QP, :]).then_inc(S.sy, 16)
    sp.wait_ge(S.sy, 64)
    g.wait_ge(S.lsem, lcount)
